import numpy as np
import ml_dtypes


def mxq(x, axis, fmt="e4m3"):
    dtype, down = {"e4m3": (ml_dtypes.float8_e4m3fn, 7), "e5m2": (ml_dtypes.float8_e5m2, 14)}[fmt]
    v = np.moveaxis(np.asarray(x, np.float32).astype(ml_dtypes.bfloat16).astype(np.float64), axis, -1)
    blocks = v.reshape(v.shape[:-1] + (-1, 32))
    amax = np.abs(blocks).max(-1, keepdims=True)
    byte = np.maximum(np.where(amax > 0, np.frexp(amax)[1] - 1 + 127, 0) - down, 1)
    scale = np.exp2(byte - 127.0)
    codes = (blocks / scale).astype(np.float32).astype(dtype).astype(np.float64)
    return np.moveaxis((codes * scale).reshape(v.shape), -1, axis)


WIDE = False


def mx_kscale(k):
    if not WIDE:
        return np.ones(k)
    levels = np.array([30, -30])
    if k % 512:
        return np.exp2(np.random.permutation(np.resize(levels, k // 32))).repeat(32)
    a = np.empty((k // 512, 16))
    for p in range(k // 512):
        a[p, :8] = np.random.permutation(np.resize(levels, 8))
        for g in range(8):
            far = levels[np.abs(levels - a[p, g]) >= 10]
            a[p, g + 8] = far[np.random.randint(len(far))]
    return np.exp2(a.ravel()).repeat(32)


def f64(x):
    return np.asarray(x).astype(np.float64)


def striped(idx):
    return np.tile(np.asarray(idx).reshape(-1, 16).T, (8, 1)).astype(np.uint16)


def unstriped(offs):
    return offs[:16].T.reshape(-1).astype(np.int64)


E2M1 = np.array([0.0, 0.5, 1.0, 1.5, 2.0, 3.0, 4.0, 6.0, -0.0, -0.5, -1.0, -1.5, -2.0, -3.0, -4.0, -6.0])


def pack_weight(w, fmt):
    k, n = w.shape
    w = f64(np.asarray(w, np.float32).astype(ml_dtypes.bfloat16)).reshape(k // 32, 32, n)
    amax = np.abs(w).max(1)
    if fmt == "e4m3":
        byte = np.frexp(amax)[1] - 1 + 127 - 7
    else:
        mant, ex = np.frexp(amax / 6.0)
        byte = np.where(mant > 0.5, ex, ex - 1) + 127
    byte = np.clip(np.where(amax > 0, byte, 1), 1, 254)
    scaled = (w * np.exp2(127.0 - byte)[:, None, :]).reshape(k, n).astype(np.float32)
    by_word = np.ascontiguousarray(scaled.reshape(k // 512, 128, 4, n).transpose(0, 1, 3, 2))
    if fmt == "e4m3":
        words = by_word.astype(ml_dtypes.float8_e4m3fn).view(np.uint8)
    else:
        c = by_word.astype(ml_dtypes.float4_e2m1fn).view(np.uint8) & 0xF
        words = (c[..., 0::2] | (c[..., 1::2] << 4)).reshape(k // 512, 128, 2 * n)
    return np.ascontiguousarray(words), np.ascontiguousarray(byte.astype(np.uint8).reshape(k // 512, 16, n))


def unpack_weight(words, scales, fmt):
    g, _, n = scales.shape
    words = np.ascontiguousarray(words).reshape(g, 128, n, -1)
    if fmt == "e4m3":
        vals = words.view(ml_dtypes.float8_e4m3fn).astype(np.float64)
    else:
        nib = np.empty((g, 128, n, 4), np.uint8)
        nib[..., 0::2] = words & 0xF
        nib[..., 1::2] = words >> 4
        vals = E2M1[nib]
    vals = vals * np.repeat(np.exp2(scales.astype(np.float64) - 127.0), 8, axis=1)[..., None]
    return vals.transpose(0, 1, 3, 2).reshape(g * 512, n)


K, T, J, I, L, S, R, O, N = 512, 512, 256, 128, 128, 512, 512, 128, 256


def setup_inputs():
    n = np.random.standard_normal
    idx = np.random.permutation(T)[:I]
    idx2 = np.random.permutation(S)[:L]
    idx3 = np.random.permutation(J)[:O]
    idx4 = np.random.permutation(J)[:O]
    fk = mx_kscale(K)
    fr = mx_kscale(R)
    wp = pack_weight(n((K, R)) * 1 / np.sqrt(K) * fk[:, None] * fr, "e2m1")
    wbp = pack_weight(n((R, N)) * 1 / np.sqrt(R) / fr[:, None], "e4m3")
    return {
        "xa": (n((K, T)) / fk[:, None]).astype(np.float32),
        "xb": (n((K, S)) * 0.6 / fk[:, None]).astype(np.float32),
        "w_words": wp[0],
        "w_scales": wp[1],
        "wb_words": wbp[0],
        "wb_scales": wbp[1],
        "rs": (n((N, O))).astype(np.float32),
        "offs": striped(idx),
        "offs2": striped(idx2),
        "offs3": striped(idx3),
        "offs4": striped(idx4),
    }


def reference(xa, xb, w_words, w_scales, wb_words, wb_scales, rs, offs, offs2, offs3, offs4):
    idx = unstriped(offs)
    idx2 = unstriped(offs2)
    idx3 = unstriped(offs3)
    idx4 = unstriped(offs4)
    wu = unpack_weight(w_words, w_scales, "e2m1")
    wbu = unpack_weight(wb_words, wb_scales, "e4m3")
    u = np.concatenate([f64(xa)[:, idx], f64(xb)[:, idx2]], axis=1)
    uq = mxq(u, 0, "e4m3")
    a = wu.T @ uq
    hid = np.maximum(a[:, idx3], a[:, idx4])
    hidq = mxq(hid, 0, "e5m2")
    p = wbu.T @ hidq
    p1 = np.pad(p, ((0, 0), (1, 0)))[:, :O]
    y = p - 0.7 * p1 + 0.5 * f64(rs)
    return y

@@ -1,0 +1,167 @@
+from contextlib import ExitStack
+
+import concourse.mybir as mybir
+
+K, T, J, HALF_J, R, O, N = 512, 512, 256, 128, 512, 128, 256
+FLOPS = 2 * K * R * J + 2 * R * N * O
+
+F32 = mybir.dt.float32
+BF16 = mybir.dt.bfloat16
+I32 = mybir.dt.int32
+U32 = mybir.dt.uint32
+U16 = mybir.dt.uint16
+U8 = mybir.dt.uint8
+E4M3 = mybir.dt.float8_e4m3fn_x4
+E5M2 = mybir.dt.float8_e5m2_x4
+E2M1 = mybir.dt.float4_e2m1fn_x4
+COPY = mybir.ActivationFunctionType.Copy
+ALU = mybir.AluOpType
+
+P = 128
+PACK = 4
+
+
+def load_scale_rows(queue, plane, scales):
+    for q in range(4):
+        queue.dma_start(
+            out=plane[32 * q : 32 * q + 4, :].bitcast(I32),
+            in_=scales[0, 4 * q : 4 * q + 4, :].bitcast(I32),
+        )
+
+
+def tile_list_looks_joined_larger_lagged_kernel(
+    tc, xa, xb, w_words, w_scales, wb_words, wb_scales, rs, offs, offs2, offs3, offs4, out
+):
+    nc = tc.nc
+    with ExitStack() as ctx:
+        sb = ctx.enter_context(tc.tile_pool(name="sb", bufs=1))
+        ps = ctx.enter_context(tc.psum_pool(name="ps", bufs=1))
+
+        list_a = sb.tile([P, 8], U16, name="list_a")
+        list_b = sb.tile([P, 8], U16, name="list_b")
+        list_3 = sb.tile([P, 8], U16, name="list_3")
+        list_4 = sb.tile([P, 8], U16, name="list_4")
+
+        w_raw = sb.tile([P, 2 * R], U8, name="w_raw", align_bytes=64)
+        w_scale_raw = sb.tile([P, R], U8, name="w_scale_raw", align_bytes=64)
+        wb_codes = sb.tile([P, N], U32, name="wb_codes", align_bytes=64)
+        wb_scale = sb.tile([P, N], U8, name="wb_scale", align_bytes=64)
+        xa_pairs = [sb.tile([P, 2, T], F32, name="xa_pair%d" % i) for i in range(2)]
+        xb_pair = sb.tile([P, 2, T], F32, name="xb_pair")
+        xb_last = [sb.tile([P, T], F32, name="xb_plane%d" % i) for i in (2, 3)]
+        rs_sb = sb.tile([P, 2, O], F32, name="rs_sb")
+
+        nc.vector.memset(w_scale_raw[:].bitcast(I32), 0)
+        nc.vector.memset(wb_scale[:].bitcast(I32), 0)
+
+        xa_rows = xa.rearrange("(p t) c -> p t c", t=PACK)
+        xb_rows = xb.rearrange("(p t) c -> p t c", t=PACK)
+        nc.sync.dma_start(out=w_raw[:].bitcast(I32), in_=w_words[0].bitcast(I32))
+        nc.sync.dma_start(out=xa_pairs[0][:], in_=xa_rows[:, 0:2, :])
+        load_scale_rows(nc.sync, w_scale_raw, w_scales)
+        nc.sync.dma_start(list_a[:], offs)
+        nc.sync.dma_start(out=xa_pairs[1][:], in_=xa_rows[:, 2:4, :])
+        nc.sync.dma_start(list_b[:], offs2)
+        nc.sync.dma_start(out=xb_pair[:], in_=xb_rows[:, 0:2, :])
+        nc.sync.dma_start(out=xb_last[0][:], in_=xb_rows[:, 2, :])
+        nc.sync.dma_start(out=xb_last[1][:], in_=xb_rows[:, 3, :])
+        nc.sync.dma_start(list_3[:], offs3)
+        nc.sync.dma_start(list_4[:], offs4)
+        nc.sync.dma_start(
+            out=wb_codes[:].bitcast(I32),
+            in_=wb_words[0].rearrange("p n t -> p (n t)").bitcast(I32),
+        )
+        load_scale_rows(nc.sync, wb_scale, wb_scales)
+        nc.sync.dma_start(out=rs_sb[:], in_=rs.rearrange("(h p) o -> p h o", p=P))
+
+        w_codes = sb.tile([P, 2 * R], U8, name="w_codes", align_bytes=64)
+        w_scale = sb.tile([P, R], U8, name="w_scale", align_bytes=64)
+        nc.vector.tensor_copy(
+            out=w_codes[:].bitcast(U16).rearrange("p (t m) -> p t m", t=PACK),
+            in_=w_raw[:].bitcast(U16).rearrange("p (m t) -> p t m", t=PACK),
+        )
+        nc.vector.tensor_copy(
+            out=w_scale[:].rearrange("p (t m) -> p t m", t=PACK),
+            in_=w_scale_raw[:].rearrange("p (m t) -> p t m", t=PACK),
+        )
+
+        a_sb = sb.tile([P, PACK, J], F32, name="a_sb")
+
+        def first_product(u_bf, name, banks):
+            codes = sb.tile([P, HALF_J], U32, name=name + "_codes", align_bytes=64)
+            scale = sb.tile([P, HALF_J], U8, name=name + "_scale", align_bytes=64)
+            nc.vector.quantize_mx(
+                out=codes[:].bitcast(E4M3), scales=scale[:], in_=u_bf[:].rearrange("p c t -> p (c t)")
+            )
+            for t in range(PACK):
+                nc.tensor.matmul_mx(
+                    out=banks[t],
+                    lhsT=w_codes[:, 2 * P * t : 2 * P * (t + 1)].bitcast(E2M1),
+                    lhsT_scale=w_scale[:, P * t : P * (t + 1)],
+                    rhs=codes[:].bitcast(E4M3),
+                    rhs_scale=scale[:],
+                    start=True,
+                    stop=True,
+                )
+
+        ua_f32 = sb.tile([P, PACK, HALF_J], F32, name="ua_f32")
+        for t in range(PACK):
+            nc.scalar.activation(ua_f32[:, t, :], xa_pairs[t // 2][:, t % 2, :].indirect(list_a[:]), COPY)
+        ua_bf = sb.tile([P, HALF_J, PACK], BF16, name="ua_bf", align_bytes=64)
+        nc.scalar.copy(
+            out=ua_bf[:].rearrange("p (c i) t -> p c t i", i=4),
+            in_=ua_f32[:].rearrange("p t (c i) -> p c t i", i=4),
+        )
+        bank_a = ps.tile([P, PACK, HALF_J], F32, name="bank_a")
+        first_product(ua_bf, "ua", [bank_a[:, t, :] for t in range(PACK)])
+        nc.scalar.copy(out=a_sb[:, :, 0:HALF_J], in_=bank_a[:])
+
+        ub_bf = sb.tile([P, HALF_J, PACK], BF16, name="ub_bf", align_bytes=64)
+        xb_planes = [xb_pair[:, 0, :], xb_pair[:, 1, :], xb_last[0][:], xb_last[1][:]]
+        for t in range(PACK):
+            nc.vector.tensor_copy(ub_bf[:, :, t], xb_planes[t].indirect(list_b[:]))
+        banks_b = [ps.tile([P, 2, HALF_J], F32, name="bank_b%d" % i) for i in range(2)]
+        first_product(ub_bf, "ub", [banks_b[t // 2][:, t % 2, :] for t in range(PACK)])
+        nc.vector.tensor_copy(out=a_sb[:, 0:2, HALF_J:J], in_=banks_b[0][:])
+        nc.scalar.copy(out=a_sb[:, 2:4, HALF_J:J], in_=banks_b[1][:])
+
+        pick3 = sb.tile([P, PACK, O], F32, name="pick3")
+        pick4 = sb.tile([P, PACK, O], F32, name="pick4")
+        for t in range(PACK):
+            for pick, slots in ((pick3, list_3), (pick4, list_4)):
+                if t < 2:
+                    nc.vector.tensor_copy(pick[:, t, :], a_sb[:, t, :].indirect(slots[:]))
+                else:
+                    nc.scalar.activation(pick[:, t, :], a_sb[:, t, :].indirect(slots[:]), COPY)
+        hid_bf = sb.tile([P, O, PACK], BF16, name="hid_bf", align_bytes=64)
+        nc.vector.tensor_tensor(
+            out=hid_bf[:].rearrange("p (c i) t -> p c t i", i=4),
+            in0=pick3[:].rearrange("p t (c i) -> p c t i", i=4),
+            in1=pick4[:].rearrange("p t (c i) -> p c t i", i=4),
+            op=ALU.max,
+        )
+        hid_codes = sb.tile([P, O], U32, name="hid_codes", align_bytes=64)
+        hid_scale = sb.tile([P, O], U8, name="hid_scale", align_bytes=64)
+        nc.vector.quantize_mx(
+            out=hid_codes[:].bitcast(E5M2), scales=hid_scale[:], in_=hid_bf[:].rearrange("p c t -> p (c t)")
+        )
+
+        for h, queue in ((0, nc.sync), (1, nc.scalar)):
+            prod = ps.tile([P, O], F32, name="prod%d" % h)
+            nc.tensor.matmul_mx(
+                out=prod[:],
+                lhsT=wb_codes[:, P * h : P * (h + 1)].bitcast(E4M3),
+                lhsT_scale=wb_scale[:, P * h : P * (h + 1)],
+                rhs=hid_codes[:].bitcast(E5M2),
+                rhs_scale=hid_scale[:],
+                start=True,
+                stop=True,
+            )
+            y = sb.tile([P, O], F32, name="y%d" % h)
+            nc.vector.scalar_tensor_tensor(
+                out=y[:], in0=rs_sb[:, h, :], scalar=0.5, in1=prod[:], op0=ALU.mult, op1=ALU.add
+            )
+            nc.vector.scalar_tensor_tensor(
+                out=y[:, 1:O], in0=prod[:, 0 : O - 1], scalar=-0.7, in1=y[:, 1:O], op0=ALU.mult, op1=ALU.add
+            )
+            queue.dma_start(out=out[P * h : P * (h + 1), :], in_=y[:])

@@ -58,11 +58,11 @@ def tile_list_looks_joined_larger_lagged_kernel(
         xb_rows = xb.rearrange("(p t) c -> p t c", t=PACK)
         nc.sync.dma_start(out=w_raw[:].bitcast(I32), in_=w_words[0].bitcast(I32))
         nc.sync.dma_start(out=xa_pairs[0][:], in_=xa_rows[:, 0:2, :])
-        load_scale_rows(nc.sync, w_scale_raw, w_scales)
         nc.sync.dma_start(list_a[:], offs)
+        load_scale_rows(nc.sync, w_scale_raw, w_scales)
         nc.sync.dma_start(out=xa_pairs[1][:], in_=xa_rows[:, 2:4, :])
-        nc.sync.dma_start(list_b[:], offs2)
         nc.sync.dma_start(out=xb_pair[:], in_=xb_rows[:, 0:2, :])
+        nc.sync.dma_start(list_b[:], offs2)
         nc.sync.dma_start(out=xb_last[0][:], in_=xb_rows[:, 2, :])
         nc.sync.dma_start(out=xb_last[1][:], in_=xb_rows[:, 3, :])
         nc.sync.dma_start(list_3[:], offs3)
@@ -85,15 +85,13 @@ def tile_list_looks_joined_larger_lagged_kernel(
             in_=w_scale_raw[:].rearrange("p (m t) -> p t m", t=PACK),
         )
 
-        a_sb = sb.tile([P, PACK, J], F32, name="a_sb")
-
         def first_product(u_bf, name, banks):
             codes = sb.tile([P, HALF_J], U32, name=name + "_codes", align_bytes=64)
             scale = sb.tile([P, HALF_J], U8, name=name + "_scale", align_bytes=64)
             nc.vector.quantize_mx(
                 out=codes[:].bitcast(E4M3), scales=scale[:], in_=u_bf[:].rearrange("p c t -> p (c t)")
             )
-            for t in range(PACK):
+            for t in (0, 2, 1, 3):
                 nc.tensor.matmul_mx(
                     out=banks[t],
                     lhsT=w_codes[:, 2 * P * t : 2 * P * (t + 1)].bitcast(E2M1),
@@ -104,26 +102,29 @@ def tile_list_looks_joined_larger_lagged_kernel(
                     stop=True,
                 )
 
-        ua_f32 = sb.tile([P, PACK, HALF_J], F32, name="ua_f32")
-        for t in range(PACK):
-            nc.scalar.activation(ua_f32[:, t, :], xa_pairs[t // 2][:, t % 2, :].indirect(list_a[:]), COPY)
-        ua_bf = sb.tile([P, HALF_J, PACK], BF16, name="ua_bf", align_bytes=64)
-        nc.scalar.copy(
-            out=ua_bf[:].rearrange("p (c i) t -> p c t i", i=4),
-            in_=ua_f32[:].rearrange("p t (c i) -> p c t i", i=4),
-        )
+        def gather_columns(planes, columns, name, low_tag):
+            low = sb.tile([P, 2, HALF_J], F32, name=name + "_low", tag=low_tag)
+            u_bf = sb.tile([P, HALF_J, PACK], BF16, name=name + "_bf", align_bytes=64)
+            for t in range(2):
+                nc.scalar.activation(low[:, t, :], planes[t].indirect(columns[:]), COPY)
+            nc.scalar.copy(out=u_bf[:, :, 0:2], in_=low[:].rearrange("p t c -> p c t"))
+            for t in range(2, PACK):
+                nc.vector.tensor_copy(u_bf[:, :, t], planes[t].indirect(columns[:]))
+            return u_bf
+
+        ua_bf = gather_columns([xa_pairs[t // 2][:, t % 2, :] for t in range(PACK)], list_a, "ua", "ua_low")
         bank_a = ps.tile([P, PACK, HALF_J], F32, name="bank_a")
         first_product(ua_bf, "ua", [bank_a[:, t, :] for t in range(PACK)])
+        ub_bf = gather_columns([xb_pair[:, 0, :], xb_pair[:, 1, :], xb_last[0][:], xb_last[1][:]], list_b, "ub", "a_sb")
+        a_sb = sb.tile([P, PACK, J], F32, name="a_sb", tag="a_sb")
         nc.scalar.copy(out=a_sb[:, :, 0:HALF_J], in_=bank_a[:])
-
-        ub_bf = sb.tile([P, HALF_J, PACK], BF16, name="ub_bf", align_bytes=64)
-        xb_planes = [xb_pair[:, 0, :], xb_pair[:, 1, :], xb_last[0][:], xb_last[1][:]]
+        banks_b = [ps.tile([P, HALF_J], F32, name="bank_b%d" % t) for t in range(PACK)]
+        first_product(ub_bf, "ub", [bank[:] for bank in banks_b])
         for t in range(PACK):
-            nc.vector.tensor_copy(ub_bf[:, :, t], xb_planes[t].indirect(list_b[:]))
-        banks_b = [ps.tile([P, 2, HALF_J], F32, name="bank_b%d" % i) for i in range(2)]
-        first_product(ub_bf, "ub", [banks_b[t // 2][:, t % 2, :] for t in range(PACK)])
-        nc.vector.tensor_copy(out=a_sb[:, 0:2, HALF_J:J], in_=banks_b[0][:])
-        nc.scalar.copy(out=a_sb[:, 2:4, HALF_J:J], in_=banks_b[1][:])
+            if t < 2:
+                nc.vector.tensor_copy(out=a_sb[:, t, HALF_J:J], in_=banks_b[t][:])
+            else:
+                nc.scalar.copy(out=a_sb[:, t, HALF_J:J], in_=banks_b[t][:])
 
         pick3 = sb.tile([P, PACK, O], F32, name="pick3")
         pick4 = sb.tile([P, PACK, O], F32, name="pick4")

@@ -54,6 +54,10 @@ def tile_list_looks_joined_larger_lagged_kernel(
         nc.vector.memset(w_scale_raw[:].bitcast(I32), 0)
         nc.vector.memset(wb_scale[:].bitcast(I32), 0)
 
+        warm = sb.tile([P, 2], F32, name="warm")
+        nc.gpsimd.memset(warm[:, 0:1], 0.0)
+        nc.scalar.activation(warm[:, 1:2], warm[:, 0:1], COPY)
+
         xa_rows = xa.rearrange("(p t) c -> p t c", t=PACK)
         xb_rows = xb.rearrange("(p t) c -> p t c", t=PACK)
         nc.sync.dma_start(out=w_raw[:].bitcast(I32), in_=w_words[0].bitcast(I32))

from contextlib import ExitStack

import concourse.mybir as mybir

K, T, J, HALF_J, R, O, N = 512, 512, 256, 128, 512, 128, 256
FLOPS = 2 * K * R * J + 2 * R * N * O

F32 = mybir.dt.float32
BF16 = mybir.dt.bfloat16
I32 = mybir.dt.int32
U32 = mybir.dt.uint32
U16 = mybir.dt.uint16
U8 = mybir.dt.uint8
E4M3 = mybir.dt.float8_e4m3fn_x4
E5M2 = mybir.dt.float8_e5m2_x4
E2M1 = mybir.dt.float4_e2m1fn_x4
COPY = mybir.ActivationFunctionType.Copy
ALU = mybir.AluOpType

P = 128
PACK = 4


def load_scale_rows(queue, plane, scales):
    for q in range(4):
        queue.dma_start(
            out=plane[32 * q : 32 * q + 4, :].bitcast(I32),
            in_=scales[0, 4 * q : 4 * q + 4, :].bitcast(I32),
        )


def tile_list_looks_joined_larger_lagged_kernel(
    tc, xa, xb, w_words, w_scales, wb_words, wb_scales, rs, offs, offs2, offs3, offs4, out
):
    nc = tc.nc
    with ExitStack() as ctx:
        sb = ctx.enter_context(tc.tile_pool(name="sb", bufs=1))
        ps = ctx.enter_context(tc.psum_pool(name="ps", bufs=1))

        list_a = sb.tile([P, 8], U16, name="list_a")
        list_b = sb.tile([P, 8], U16, name="list_b")
        list_3 = sb.tile([P, 8], U16, name="list_3")
        list_4 = sb.tile([P, 8], U16, name="list_4")

        w_raw = sb.tile([P, 2 * R], U8, name="w_raw", align_bytes=64)
        w_scale_raw = sb.tile([P, R], U8, name="w_scale_raw", align_bytes=64)
        wb_codes = sb.tile([P, N], U32, name="wb_codes", align_bytes=64)
        wb_scale = sb.tile([P, N], U8, name="wb_scale", align_bytes=64)
        xa_pairs = [sb.tile([P, 2, T], F32, name="xa_pair%d" % i) for i in range(2)]
        xb_pair = sb.tile([P, 2, T], F32, name="xb_pair")
        xb_last = [sb.tile([P, T], F32, name="xb_plane%d" % i) for i in (2, 3)]
        rs_sb = sb.tile([P, 2, O], F32, name="rs_sb")

        nc.vector.memset(w_scale_raw[:].bitcast(I32), 0)
        nc.vector.memset(wb_scale[:].bitcast(I32), 0)

        warm = sb.tile([P, 2], F32, name="warm")
        nc.gpsimd.memset(warm[:, 0:1], 0.0)
        nc.scalar.activation(warm[:, 1:2], warm[:, 0:1], COPY)

        xa_rows = xa.rearrange("(p t) c -> p t c", t=PACK)
        xb_rows = xb.rearrange("(p t) c -> p t c", t=PACK)
        nc.sync.dma_start(out=w_raw[:].bitcast(I32), in_=w_words[0].bitcast(I32))
        nc.sync.dma_start(out=xa_pairs[0][:], in_=xa_rows[:, 0:2, :])
        nc.sync.dma_start(list_a[:], offs)
        load_scale_rows(nc.sync, w_scale_raw, w_scales)
        nc.sync.dma_start(out=xa_pairs[1][:], in_=xa_rows[:, 2:4, :])
        nc.sync.dma_start(out=xb_pair[:], in_=xb_rows[:, 0:2, :])
        nc.sync.dma_start(list_b[:], offs2)
        nc.sync.dma_start(out=xb_last[0][:], in_=xb_rows[:, 2, :])
        nc.sync.dma_start(out=xb_last[1][:], in_=xb_rows[:, 3, :])
        nc.sync.dma_start(list_3[:], offs3)
        nc.sync.dma_start(list_4[:], offs4)
        nc.sync.dma_start(
            out=wb_codes[:].bitcast(I32),
            in_=wb_words[0].rearrange("p n t -> p (n t)").bitcast(I32),
        )
        load_scale_rows(nc.sync, wb_scale, wb_scales)
        nc.sync.dma_start(out=rs_sb[:], in_=rs.rearrange("(h p) o -> p h o", p=P))

        w_codes = sb.tile([P, 2 * R], U8, name="w_codes", align_bytes=64)
        w_scale = sb.tile([P, R], U8, name="w_scale", align_bytes=64)
        nc.vector.tensor_copy(
            out=w_codes[:].bitcast(U16).rearrange("p (t m) -> p t m", t=PACK),
            in_=w_raw[:].bitcast(U16).rearrange("p (m t) -> p t m", t=PACK),
        )
        nc.vector.tensor_copy(
            out=w_scale[:].rearrange("p (t m) -> p t m", t=PACK),
            in_=w_scale_raw[:].rearrange("p (m t) -> p t m", t=PACK),
        )

        def first_product(u_bf, name, banks):
            codes = sb.tile([P, HALF_J], U32, name=name + "_codes", align_bytes=64)
            scale = sb.tile([P, HALF_J], U8, name=name + "_scale", align_bytes=64)
            nc.vector.quantize_mx(
                out=codes[:].bitcast(E4M3), scales=scale[:], in_=u_bf[:].rearrange("p c t -> p (c t)")
            )
            for t in (0, 2, 1, 3):
                nc.tensor.matmul_mx(
                    out=banks[t],
                    lhsT=w_codes[:, 2 * P * t : 2 * P * (t + 1)].bitcast(E2M1),
                    lhsT_scale=w_scale[:, P * t : P * (t + 1)],
                    rhs=codes[:].bitcast(E4M3),
                    rhs_scale=scale[:],
                    start=True,
                    stop=True,
                )

        def gather_columns(planes, columns, name, low_tag):
            low = sb.tile([P, 2, HALF_J], F32, name=name + "_low", tag=low_tag)
            u_bf = sb.tile([P, HALF_J, PACK], BF16, name=name + "_bf", align_bytes=64)
            for t in range(2):
                nc.scalar.activation(low[:, t, :], planes[t].indirect(columns[:]), COPY)
            nc.scalar.copy(out=u_bf[:, :, 0:2], in_=low[:].rearrange("p t c -> p c t"))
            for t in range(2, PACK):
                nc.vector.tensor_copy(u_bf[:, :, t], planes[t].indirect(columns[:]))
            return u_bf

        ua_bf = gather_columns([xa_pairs[t // 2][:, t % 2, :] for t in range(PACK)], list_a, "ua", "ua_low")
        bank_a = ps.tile([P, PACK, HALF_J], F32, name="bank_a")
        first_product(ua_bf, "ua", [bank_a[:, t, :] for t in range(PACK)])
        ub_bf = gather_columns([xb_pair[:, 0, :], xb_pair[:, 1, :], xb_last[0][:], xb_last[1][:]], list_b, "ub", "a_sb")
        a_sb = sb.tile([P, PACK, J], F32, name="a_sb", tag="a_sb")
        nc.scalar.copy(out=a_sb[:, :, 0:HALF_J], in_=bank_a[:])
        banks_b = [ps.tile([P, HALF_J], F32, name="bank_b%d" % t) for t in range(PACK)]
        first_product(ub_bf, "ub", [bank[:] for bank in banks_b])
        for t in range(PACK):
            if t < 2:
                nc.vector.tensor_copy(out=a_sb[:, t, HALF_J:J], in_=banks_b[t][:])
            else:
                nc.scalar.copy(out=a_sb[:, t, HALF_J:J], in_=banks_b[t][:])

        pick3 = sb.tile([P, PACK, O], F32, name="pick3")
        pick4 = sb.tile([P, PACK, O], F32, name="pick4")
        for t in range(PACK):
            for pick, slots in ((pick3, list_3), (pick4, list_4)):
                if t < 2:
                    nc.vector.tensor_copy(pick[:, t, :], a_sb[:, t, :].indirect(slots[:]))
                else:
                    nc.scalar.activation(pick[:, t, :], a_sb[:, t, :].indirect(slots[:]), COPY)
        hid_bf = sb.tile([P, O, PACK], BF16, name="hid_bf", align_bytes=64)
        nc.vector.tensor_tensor(
            out=hid_bf[:].rearrange("p (c i) t -> p c t i", i=4),
            in0=pick3[:].rearrange("p t (c i) -> p c t i", i=4),
            in1=pick4[:].rearrange("p t (c i) -> p c t i", i=4),
            op=ALU.max,
        )
        hid_codes = sb.tile([P, O], U32, name="hid_codes", align_bytes=64)
        hid_scale = sb.tile([P, O], U8, name="hid_scale", align_bytes=64)
        nc.vector.quantize_mx(
            out=hid_codes[:].bitcast(E5M2), scales=hid_scale[:], in_=hid_bf[:].rearrange("p c t -> p (c t)")
        )

        for h, queue in ((0, nc.sync), (1, nc.scalar)):
            prod = ps.tile([P, O], F32, name="prod%d" % h)
            nc.tensor.matmul_mx(
                out=prod[:],
                lhsT=wb_codes[:, P * h : P * (h + 1)].bitcast(E4M3),
                lhsT_scale=wb_scale[:, P * h : P * (h + 1)],
                rhs=hid_codes[:].bitcast(E5M2),
                rhs_scale=hid_scale[:],
                start=True,
                stop=True,
            )
            y = sb.tile([P, O], F32, name="y%d" % h)
            nc.vector.scalar_tensor_tensor(
                out=y[:], in0=rs_sb[:, h, :], scalar=0.5, in1=prod[:], op0=ALU.mult, op1=ALU.add
            )
            nc.vector.scalar_tensor_tensor(
                out=y[:, 1:O], in0=prod[:, 0 : O - 1], scalar=-0.7, in1=y[:, 1:O], op0=ALU.mult, op1=ALU.add
            )
            queue.dma_start(out=out[P * h : P * (h + 1), :], in_=y[:])
